import numpy as np, ml_dtypes
CORES = [66,74,82,90,194,202,210,218]
N = 8
TK, NT = 512, 4
def setup_inputs(rng):
    x = rng.standard_normal((NT, 128, TK), dtype=np.float32).astype(ml_dtypes.bfloat16)
    return {"x": np.broadcast_to(x, (2, NT, 128, TK)).reshape(N, 128, TK).copy(), "w": rng.standard_normal((N, 128, NT * 128), dtype=np.float32).astype(ml_dtypes.bfloat16)}
def setup_inputs_big(rng):
    d = setup_inputs(rng)
    for k in ("x", "w"): d[k] = (d[k].astype(np.float32) * 1024.0).astype(d[k].dtype)
    return d
def setup_inputs_small(rng):
    d = setup_inputs(rng)
    for k in ("x", "w"): d[k] = (d[k].astype(np.float32) * (1 / 1024.0)).astype(d[k].dtype)
    return d
def setup_inputs_apart(rng):
    d = setup_inputs(rng)
    f = (10.0 ** rng.permutation(np.linspace(-1.5, 1.5, N))).astype(np.float32).reshape(N, 1, 1)
    for k in ("x", "w"): d[k] = (d[k].astype(np.float32) * f).astype(d[k].dtype)
    return d
def reference(x, w):
    X, W = x.astype(np.float64), w.astype(np.float64)
    y = np.stack([sum(W[r][:, 128 * j:128 * j + 128].T @ X[j if r < NT else j + NT] for j in range(NT)) for r in range(N)])
    return {"y": y.astype(ml_dtypes.bfloat16)}

@@ -1,0 +1,82 @@
+from concourse.bass import DstId, RemoteDMATransfer
+
+NT, TK, M = 4, 512, 128
+H = TK // 2
+
+SCRATCH = {
+    "xs": ("sbuf", [128, NT * TK], "bfloat16"),
+    "ws": ("sbuf", [128, NT * M], "bfloat16"),
+    "ys": ("sbuf", [128, TK], "bfloat16"),
+    "acc0": ("psum", [128, 512], "float32"),
+    "acc1": ("psum", [128, 512], "float32"),
+}
+SEMAPHORES = ["xl", "wl", "a0", "a1", "a2", "a3", "sent", "m0", "m1", "c0", "c1", "s0", "s1"]
+
+
+def _links(topo, src, dst):
+    return 1 if (topo.mates(src, dst) or topo.same_plane(src, dst)) else 2
+
+
+def _source(T, topo, dst, j):
+    holders = [c for i, c in enumerate(T.cores) if i % NT == j]
+    return min(holders, key=lambda c: (_links(topo, c, dst), topo.host(c) != topo.host(dst)))
+
+
+def _bits(mask):
+    return sum(1 for e in range(16) if (mask >> e) & 1)
+
+
+def rank_program(g, core, T, topo):
+    rank = T.rank_of(core)
+    if rank is None:
+        return
+    own = rank % NT
+    slot = lambda j: T.xs[:, j * TK:(j + 1) * TK]
+
+    g.sync.dma_start(slot(own), T.x[:, :]).then_inc(T.sem.xl, 16)
+    g.scalar.dma_start(T.ws[:, :], T.w[:, :]).then_inc(T.sem.wl, 16)
+
+    dests = [d for i, d in enumerate(T.cores) if i % NT != own and _source(T, topo, d, own) == core]
+    dests.sort(key=lambda d: -_links(topo, core, d))
+    mask = topo.mask(core, dests[0])
+    for d in dests:
+        mask &= topo.mask(core, d)
+    ids = []
+    for d in dests:
+        rid, pid = topo.addr(d, core)
+        ids.append(DstId(rid=rid, pnc=pid))
+    g.wait_ge(T.sem.xl, 16)
+    g.remote_dma_fused(
+        [RemoteDMATransfer(dst_ids=ids, dma_engine_mask=mask, remote_sem=T.sem["a%d" % own],
+                           srcs=[slot(own)], dsts=[slot(own) for _ in dests])],
+        local_sem=T.sem.sent)
+
+    order = [j for j in range(NT) if j != own]
+    order.sort(key=lambda j: -_links(topo, _source(T, topo, core, j), core))
+    g.tensor.wait_ge(T.sem.xl, 16)
+    g.tensor.wait_ge(T.sem.wl, 16)
+    seq = [own] + order
+    for k, j in enumerate(seq):
+        if j != own:
+            g.tensor.wait_ge(T.sem["a%d" % j], _bits(topo.mask(_source(T, topo, core, j), core)))
+        first, last = k == 0, k == len(seq) - 1
+        wt = T.ws[:, j * M:(j + 1) * M]
+        i0 = g.tensor.matmul(T.acc0[:, 0:H], wt, T.xs[:, j * TK:j * TK + H], first, last)
+        if last:
+            i0.then_inc(T.sem.m0, 1)
+        i1 = g.tensor.matmul(T.acc1[:, 0:H], wt, T.xs[:, j * TK + H:(j + 1) * TK], first, last)
+        if last:
+            i1.then_inc(T.sem.m1, 1)
+
+    g.vector.wait_ge(T.sem.m0, 1)
+    g.vector.tensor_copy(T.ys[:, 0:H], T.acc0[:, 0:H]).then_inc(T.sem.c0, 1)
+    g.vector.wait_ge(T.sem.m1, 1)
+    g.vector.tensor_copy(T.ys[:, H:TK], T.acc1[:, 0:H]).then_inc(T.sem.c1, 1)
+    g.sync.wait_ge(T.sem.c0, 1)
+    g.sync.dma_start(T.y[:, 0:H], T.ys[:, 0:H]).then_inc(T.sem.s0, 16)
+    g.scalar.wait_ge(T.sem.c1, 1)
+    g.scalar.dma_start(T.y[:, H:TK], T.ys[:, H:TK]).then_inc(T.sem.s1, 16)
+
+    g.wait_ge(T.sem.sent, _bits(mask))
+    g.sync.wait_ge(T.sem.s0, 16)
+    g.scalar.wait_ge(T.sem.s1, 16)

@@ -1,7 +1,8 @@
 from concourse.bass import DstId, RemoteDMATransfer
 
 NT, TK, M = 4, 512, 128
-H = TK // 2
+NH = 2
+H = TK // NH
 
 SCRATCH = {
     "xs": ("sbuf", [128, NT * TK], "bfloat16"),
@@ -10,11 +11,16 @@ SCRATCH = {
     "acc0": ("psum", [128, 512], "float32"),
     "acc1": ("psum", [128, 512], "float32"),
 }
-SEMAPHORES = ["xl", "wl", "a0", "a1", "a2", "a3", "sent", "m0", "m1", "c0", "c1", "s0", "s1"]
+SEMAPHORES = (["xl0", "xl1", "wl", "sent", "m0", "m1", "c0", "c1", "s0", "s1"]
+              + ["a%d_%d" % (j, h) for j in range(NT) for h in range(NH)])
 
 
 def _links(topo, src, dst):
     return 1 if (topo.mates(src, dst) or topo.same_plane(src, dst)) else 2
+
+
+def _turn(topo, src, dst):
+    return (-_links(topo, src, dst), 1 if topo.mates(src, dst) else 0)
 
 
 def _source(T, topo, dst, j):
@@ -31,13 +37,16 @@ def rank_program(g, core, T, topo):
     if rank is None:
         return
     own = rank % NT
-    slot = lambda j: T.xs[:, j * TK:(j + 1) * TK]
+    piece = lambda j, h: T.xs[:, j * TK + h * H:j * TK + (h + 1) * H]
+    cols = lambda t, h: t[:, h * H:(h + 1) * H]
+    queue = [g.sync, g.scalar]
 
-    g.sync.dma_start(slot(own), T.x[:, :]).then_inc(T.sem.xl, 16)
-    g.scalar.dma_start(T.ws[:, :], T.w[:, :]).then_inc(T.sem.wl, 16)
+    for h in range(NH):
+        queue[h].dma_start(piece(own, h), cols(T.x, h)).then_inc(T.sem["xl%d" % h], 16)
+    g.sync.dma_start(T.ws[:, :], T.w[:, :]).then_inc(T.sem.wl, 16)
 
     dests = [d for i, d in enumerate(T.cores) if i % NT != own and _source(T, topo, d, own) == core]
-    dests.sort(key=lambda d: -_links(topo, core, d))
+    dests.sort(key=lambda d: _turn(topo, core, d))
     mask = topo.mask(core, dests[0])
     for d in dests:
         mask &= topo.mask(core, d)
@@ -45,38 +54,35 @@ def rank_program(g, core, T, topo):
     for d in dests:
         rid, pid = topo.addr(d, core)
         ids.append(DstId(rid=rid, pnc=pid))
-    g.wait_ge(T.sem.xl, 16)
-    g.remote_dma_fused(
-        [RemoteDMATransfer(dst_ids=ids, dma_engine_mask=mask, remote_sem=T.sem["a%d" % own],
-                           srcs=[slot(own)], dsts=[slot(own) for _ in dests])],
-        local_sem=T.sem.sent)
+    for h in range(NH):
+        g.wait_ge(T.sem["xl%d" % h], 16)
+        g.remote_dma_fused(
+            [RemoteDMATransfer(dst_ids=ids, dma_engine_mask=mask, remote_sem=T.sem["a%d_%d" % (own, h)],
+                               srcs=[piece(own, h)], dsts=[piece(own, h) for _ in dests])],
+            local_sem=T.sem.sent)
 
     order = [j for j in range(NT) if j != own]
-    order.sort(key=lambda j: -_links(topo, _source(T, topo, core, j), core))
-    g.tensor.wait_ge(T.sem.xl, 16)
+    order.sort(key=lambda j: _turn(topo, _source(T, topo, core, j), core))
+    acc = [T.acc0, T.acc1]
+    tile = lambda j: T.ws[:, j * M:(j + 1) * M]
     g.tensor.wait_ge(T.sem.wl, 16)
-    seq = [own] + order
-    for k, j in enumerate(seq):
-        if j != own:
-            g.tensor.wait_ge(T.sem["a%d" % j], _bits(topo.mask(_source(T, topo, core, j), core)))
-        first, last = k == 0, k == len(seq) - 1
-        wt = T.ws[:, j * M:(j + 1) * M]
-        i0 = g.tensor.matmul(T.acc0[:, 0:H], wt, T.xs[:, j * TK:j * TK + H], first, last)
-        if last:
-            i0.then_inc(T.sem.m0, 1)
-        i1 = g.tensor.matmul(T.acc1[:, 0:H], wt, T.xs[:, j * TK + H:(j + 1) * TK], first, last)
-        if last:
-            i1.then_inc(T.sem.m1, 1)
+    for h in range(NH):
+        g.tensor.wait_ge(T.sem["xl%d" % h], 16)
+        g.tensor.matmul(acc[h][:, 0:H], tile(own), piece(own, h), True, False)
+    for h in range(NH):
+        for j in order:
+            g.tensor.wait_ge(T.sem["a%d_%d" % (j, h)], _bits(topo.mask(_source(T, topo, core, j), core)))
+            last = j == order[-1]
+            i = g.tensor.matmul(acc[h][:, 0:H], tile(j), piece(j, h), False, last)
+            if last:
+                i.then_inc(T.sem["m%d" % h], 1)
 
-    g.vector.wait_ge(T.sem.m0, 1)
-    g.vector.tensor_copy(T.ys[:, 0:H], T.acc0[:, 0:H]).then_inc(T.sem.c0, 1)
-    g.vector.wait_ge(T.sem.m1, 1)
-    g.vector.tensor_copy(T.ys[:, H:TK], T.acc1[:, 0:H]).then_inc(T.sem.c1, 1)
-    g.sync.wait_ge(T.sem.c0, 1)
-    g.sync.dma_start(T.y[:, 0:H], T.ys[:, 0:H]).then_inc(T.sem.s0, 16)
-    g.scalar.wait_ge(T.sem.c1, 1)
-    g.scalar.dma_start(T.y[:, H:TK], T.ys[:, H:TK]).then_inc(T.sem.s1, 16)
+    for h in range(NH):
+        g.vector.wait_ge(T.sem["m%d" % h], 1)
+        g.vector.tensor_copy(cols(T.ys, h), acc[h][:, 0:H]).then_inc(T.sem["c%d" % h], 1)
+        queue[h].wait_ge(T.sem["c%d" % h], 1)
+        queue[h].dma_start(cols(T.y, h), cols(T.ys, h)).then_inc(T.sem["s%d" % h], 16)
 
-    g.wait_ge(T.sem.sent, _bits(mask))
-    g.sync.wait_ge(T.sem.s0, 16)
-    g.scalar.wait_ge(T.sem.s1, 16)
+    g.wait_ge(T.sem.sent, NH * _bits(mask))
+    for h in range(NH):
+        queue[h].wait_ge(T.sem["s%d" % h], 16)

from concourse.bass import DstId, RemoteDMATransfer

NT, TK, M = 4, 512, 128
NH = 2
H = TK // NH

SCRATCH = {
    "xs": ("sbuf", [128, NT * TK], "bfloat16"),
    "ws": ("sbuf", [128, NT * M], "bfloat16"),
    "ys": ("sbuf", [128, TK], "bfloat16"),
    "acc0": ("psum", [128, 512], "float32"),
    "acc1": ("psum", [128, 512], "float32"),
}
SEMAPHORES = (["xl0", "xl1", "wl", "sent", "m0", "m1", "c0", "c1", "s0", "s1"]
              + ["a%d_%d" % (j, h) for j in range(NT) for h in range(NH)])


def _links(topo, src, dst):
    return 1 if (topo.mates(src, dst) or topo.same_plane(src, dst)) else 2


def _turn(topo, src, dst):
    return (-_links(topo, src, dst), 1 if topo.mates(src, dst) else 0)


def _source(T, topo, dst, j):
    holders = [c for i, c in enumerate(T.cores) if i % NT == j]
    return min(holders, key=lambda c: (_links(topo, c, dst), topo.host(c) != topo.host(dst)))


def _bits(mask):
    return sum(1 for e in range(16) if (mask >> e) & 1)


def rank_program(g, core, T, topo):
    rank = T.rank_of(core)
    if rank is None:
        return
    own = rank % NT
    piece = lambda j, h: T.xs[:, j * TK + h * H:j * TK + (h + 1) * H]
    cols = lambda t, h: t[:, h * H:(h + 1) * H]
    queue = [g.sync, g.scalar]

    for h in range(NH):
        queue[h].dma_start(piece(own, h), cols(T.x, h)).then_inc(T.sem["xl%d" % h], 16)
    g.sync.dma_start(T.ws[:, :], T.w[:, :]).then_inc(T.sem.wl, 16)

    dests = [d for i, d in enumerate(T.cores) if i % NT != own and _source(T, topo, d, own) == core]
    dests.sort(key=lambda d: _turn(topo, core, d))
    mask = topo.mask(core, dests[0])
    for d in dests:
        mask &= topo.mask(core, d)
    ids = []
    for d in dests:
        rid, pid = topo.addr(d, core)
        ids.append(DstId(rid=rid, pnc=pid))
    for h in range(NH):
        g.wait_ge(T.sem["xl%d" % h], 16)
        g.remote_dma_fused(
            [RemoteDMATransfer(dst_ids=ids, dma_engine_mask=mask, remote_sem=T.sem["a%d_%d" % (own, h)],
                               srcs=[piece(own, h)], dsts=[piece(own, h) for _ in dests])],
            local_sem=T.sem.sent)

    order = [j for j in range(NT) if j != own]
    order.sort(key=lambda j: _turn(topo, _source(T, topo, core, j), core))
    acc = [T.acc0, T.acc1]
    tile = lambda j: T.ws[:, j * M:(j + 1) * M]
    g.tensor.wait_ge(T.sem.wl, 16)
    for h in range(NH):
        g.tensor.wait_ge(T.sem["xl%d" % h], 16)
        g.tensor.matmul(acc[h][:, 0:H], tile(own), piece(own, h), True, False)
    for h in range(NH):
        for j in order:
            g.tensor.wait_ge(T.sem["a%d_%d" % (j, h)], _bits(topo.mask(_source(T, topo, core, j), core)))
            last = j == order[-1]
            i = g.tensor.matmul(acc[h][:, 0:H], tile(j), piece(j, h), False, last)
            if last:
                i.then_inc(T.sem["m%d" % h], 1)

    for h in range(NH):
        g.vector.wait_ge(T.sem["m%d" % h], 1)
        g.vector.tensor_copy(cols(T.ys, h), acc[h][:, 0:H]).then_inc(T.sem["c%d" % h], 1)
        queue[h].wait_ge(T.sem["c%d" % h], 1)
        queue[h].dma_start(cols(T.y, h), cols(T.ys, h)).then_inc(T.sem["s%d" % h], 16)

    g.wait_ge(T.sem.sent, NH * _bits(mask))
    for h in range(NH):
        queue[h].wait_ge(T.sem["s%d" % h], 16)
